import numpy as np
import ml_dtypes


def mxq(x, axis, fmt="e4m3"):
    dtype, down = {"e4m3": (ml_dtypes.float8_e4m3fn, 7), "e5m2": (ml_dtypes.float8_e5m2, 14)}[fmt]
    v = np.moveaxis(np.asarray(x, np.float32).astype(ml_dtypes.bfloat16).astype(np.float64), axis, -1)
    blocks = v.reshape(v.shape[:-1] + (-1, 32))
    amax = np.abs(blocks).max(-1, keepdims=True)
    byte = np.maximum(np.where(amax > 0, np.frexp(amax)[1] - 1 + 127, 0) - down, 1)
    scale = np.exp2(byte - 127.0)
    codes = (blocks / scale).astype(np.float32).astype(dtype).astype(np.float64)
    return np.moveaxis((codes * scale).reshape(v.shape), -1, axis)


WIDE = False


def mx_kscale(k):
    if not WIDE:
        return np.ones(k)
    levels = np.array([30, -30])
    if k % 512:
        return np.exp2(np.random.permutation(np.resize(levels, k // 32))).repeat(32)
    a = np.empty((k // 512, 16))
    for p in range(k // 512):
        a[p, :8] = np.random.permutation(np.resize(levels, 8))
        for g in range(8):
            far = levels[np.abs(levels - a[p, g]) >= 10]
            a[p, g + 8] = far[np.random.randint(len(far))]
    return np.exp2(a.ravel()).repeat(32)


def f64(x):
    return np.asarray(x).astype(np.float64)


def striped(idx):
    return np.tile(np.asarray(idx).reshape(-1, 16).T, (8, 1)).astype(np.uint16)


def unstriped(offs):
    return offs[:16].T.reshape(-1).astype(np.int64)


E2M1 = np.array([0.0, 0.5, 1.0, 1.5, 2.0, 3.0, 4.0, 6.0, -0.0, -0.5, -1.0, -1.5, -2.0, -3.0, -4.0, -6.0])


def pack_weight(w, fmt):
    k, n = w.shape
    w = f64(np.asarray(w, np.float32).astype(ml_dtypes.bfloat16)).reshape(k // 32, 32, n)
    amax = np.abs(w).max(1)
    if fmt in ("e4m3", "e5m2"):
        byte = np.frexp(amax)[1] - 1 + 127 - (7 if fmt == "e4m3" else 14)
    else:
        mant, ex = np.frexp(amax / 6.0)
        byte = np.where(mant > 0.5, ex, ex - 1) + 127
    byte = np.clip(np.where(amax > 0, byte, 1), 1, 254)
    scaled = (w * np.exp2(127.0 - byte)[:, None, :]).reshape(k, n).astype(np.float32)
    by_word = np.ascontiguousarray(scaled.reshape(k // 512, 128, 4, n).transpose(0, 1, 3, 2))
    if fmt in ("e4m3", "e5m2"):
        words = by_word.astype(ml_dtypes.float8_e4m3fn if fmt == "e4m3" else ml_dtypes.float8_e5m2).view(np.uint8)
    else:
        c = by_word.astype(ml_dtypes.float4_e2m1fn).view(np.uint8) & 0xF
        words = (c[..., 0::2] | (c[..., 1::2] << 4)).reshape(k // 512, 128, 2 * n)
    return np.ascontiguousarray(words), np.ascontiguousarray(byte.astype(np.uint8).reshape(k // 512, 16, n))


def unpack_weight(words, scales, fmt):
    g, _, n = scales.shape
    words = np.ascontiguousarray(words).reshape(g, 128, n, -1)
    if fmt in ("e4m3", "e5m2"):
        vals = words.view(ml_dtypes.float8_e4m3fn if fmt == "e4m3" else ml_dtypes.float8_e5m2).astype(np.float64)
    else:
        nib = np.empty((g, 128, n, 4), np.uint8)
        nib[..., 0::2] = words & 0xF
        nib[..., 1::2] = words >> 4
        vals = E2M1[nib]
    vals = vals * np.repeat(np.exp2(scales.astype(np.float64) - 127.0), 8, axis=1)[..., None]
    return vals.transpose(0, 1, 3, 2).reshape(g * 512, n)


def sigmoid(v):
    return 1.0 / (1.0 + np.exp(-v))


K, T, J, R, C, O, N, L, E = 512, 2048, 256, 512, 512, 256, 256, 512, 1024


def setup_inputs():
    n = np.random.standard_normal
    idx = np.random.permutation(T)[:J]
    idx2 = np.random.permutation(T)[:J]
    idx3 = np.random.permutation(C)[:J]
    idx4 = np.random.permutation(C)[:J]
    idx5 = np.random.permutation(C)[:O]
    idx6 = np.random.permutation(C)[:O]
    idx7 = np.random.permutation(E)[:O]
    fk = mx_kscale(K)
    fr = mx_kscale(R)
    fl = mx_kscale(L)
    xtp = pack_weight(n((K, T)) / fk[:, None], "e4m3")
    wp = pack_weight(n((K, R)) * 1 / np.sqrt(K) * fk[:, None] * fr, "e2m1")
    wbp = pack_weight(n((R, N)) * 1 / np.sqrt(R) / fr[:, None], "e5m2")
    sxp = pack_weight(n((L, O)) / fl[:, None], "e2m1")
    wsp = pack_weight(n((L, N)) * 1 / np.sqrt(L) * fl[:, None], "e5m2")
    return {
        "xt_words": xtp[0],
        "xt_scales": xtp[1],
        "w_words": wp[0],
        "w_scales": wp[1],
        "wb_words": wbp[0],
        "wb_scales": wbp[1],
        "sx_words": sxp[0],
        "sx_scales": sxp[1],
        "ws_words": wsp[0],
        "ws_scales": wsp[1],
        "tz": (n((N, E))).astype(np.float32),
        "so": (np.random.uniform(0.6, 1.6, (N, 1))).astype(np.float32),
        "bo": (np.random.uniform(-1.0, 1.0, (N, 1))).astype(np.float32),
        "offs": striped(idx),
        "offs2": striped(idx2),
        "offs3": striped(idx3),
        "offs4": striped(idx4),
        "offs5": striped(idx5),
        "offs6": striped(idx6),
        "offs7": striped(idx7),
    }


def reference(xt_words, xt_scales, w_words, w_scales, wb_words, wb_scales, sx_words, sx_scales, ws_words, ws_scales, tz, so, bo, offs, offs2, offs3, offs4, offs5, offs6, offs7):
    idx = unstriped(offs)
    idx2 = unstriped(offs2)
    idx3 = unstriped(offs3)
    idx4 = unstriped(offs4)
    idx5 = unstriped(offs5)
    idx6 = unstriped(offs6)
    idx7 = unstriped(offs7)
    xtu = unpack_weight(xt_words, xt_scales, "e4m3")
    wu = unpack_weight(w_words, w_scales, "e2m1")
    wbu = unpack_weight(wb_words, wb_scales, "e5m2")
    sxu = unpack_weight(sx_words, sx_scales, "e2m1")
    wsu = unpack_weight(ws_words, ws_scales, "e5m2")
    xtidxg = xtu[:, idx]
    a = wu.T @ xtidxg
    xtidx2g = xtu[:, idx2]
    b = wu.T @ xtidx2g
    pw = np.zeros((R, C))
    pw[:, idx3] = a
    pv = np.zeros((R, C))
    pv[:, idx4] = b
    hid = np.abs(pw[:, idx5] - pv[:, idx6])
    hidq = mxq(hid, 0, "e4m3")
    p = wbu.T @ hidq + wsu.T @ sxu
    y = p * sigmoid(f64(tz)[:, idx7] * f64(so) + f64(bo))
    return y

@@ -1,0 +1,170 @@
+from contextlib import ExitStack
+
+import concourse.mybir as mybir
+
+K, T, J, R, C, O, N, L, E = 512, 2048, 256, 512, 512, 256, 256, 512, 1024
+FLOPS = 2 * (2 * K * R * J + R * N * O + L * N * O)
+
+F32 = mybir.dt.float32
+BF16 = mybir.dt.bfloat16
+I32 = mybir.dt.int32
+U32 = mybir.dt.uint32
+U16 = mybir.dt.uint16
+U8 = mybir.dt.uint8
+E4M3 = mybir.dt.float8_e4m3fn_x4
+E5M2 = mybir.dt.float8_e5m2_x4
+E2M1 = mybir.dt.float4_e2m1fn_x4
+ACT = mybir.ActivationFunctionType
+ALU = mybir.AluOpType
+
+P = 128
+PACK = 4
+QUADS = 4
+
+
+def load_scales(queue, plane, scales, quads=range(QUADS)):
+    for q in quads:
+        queue.dma_start(out=plane[32 * q : 32 * q + 4, :].bitcast(I32), in_=scales[0, 4 * q : 4 * q + 4, :].bitcast(I32))
+
+
+def tile_list_tied_twoboards_skip_finalgate_kernel(
+    tc, xt_words, xt_scales, w_words, w_scales, wb_words, wb_scales, sx_words, sx_scales, ws_words, ws_scales,
+    tz, so, bo, offs, offs2, offs3, offs4, offs5, offs6, offs7, out,
+):
+    nc = tc.nc
+    with ExitStack() as ctx:
+        sb = ctx.enter_context(tc.tile_pool(name="sb", bufs=1))
+        ps = ctx.enter_context(tc.psum_pool(name="ps", bufs=1))
+
+        def tile(name, shape, dtype):
+            return sb.tile(shape, dtype, name=name, align_bytes=64)
+
+        lists = {n: tile(n, [P, J // 16], U16) for n in ("l1", "l2", "l3", "l4", "l5", "l6", "l7")}
+        xw = tile("xw", [P, T], I32)
+        xs = tile("xs", [P, T], U8)
+        ww = tile("ww", [P, R], U16)
+        wsc = tile("wsc", [P, R], U8)
+        late = tile("late", [P, 3 * N], U8)
+
+        nc.vector.memset(xs[:].bitcast(I32), 0)
+
+        nc.sync.dma_start(lists["l1"][:], offs)
+        nc.scalar.dma_start(out=ww[:].bitcast(I32), in_=w_words[0].bitcast(I32))
+        nc.sync.dma_start(lists["l2"][:], offs2)
+        load_scales(nc.scalar, xs, xt_scales, (0, 1))
+        load_scales(nc.sync, xs, xt_scales, (2, 3))
+        nc.sync.dma_start(out=xw[:], in_=xt_words[0].rearrange("p c r -> p (c r)").bitcast(I32))
+
+        pw = [tile("pw%d" % t, [P, C], F32) for t in range(PACK)]
+        pv = [tile("pv%d" % t, [P, C], F32) for t in range(PACK)]
+        for board in pw[:2]:
+            nc.vector.memset(board[:], 0.0)
+        nc.vector.memset(late[:].bitcast(I32), 0)
+        nc.vector.memset(wsc[:].bitcast(I32), 0)
+        for board in pw[2:] + pv:
+            nc.vector.memset(board[:], 0.0)
+
+        load_scales(nc.scalar, wsc, w_scales)
+        nc.sync.dma_start(lists["l3"][:], offs3)
+        nc.sync.dma_start(lists["l5"][:], offs5)
+        nc.sync.dma_start(lists["l4"][:], offs4)
+        nc.sync.dma_start(lists["l6"][:], offs6)
+
+        wsw = tile("wsw", [P, N], I32)
+        sxw = tile("sxw", [P, O], U16)
+        wbw = tile("wbw", [P, N], I32)
+        wss, sxs, wbs = late[:, 0:N], late[:, N : 2 * N], late[:, 2 * N : 3 * N]
+        nc.sync.dma_start(out=wsw[:], in_=ws_words[0].rearrange("p c r -> p (c r)").bitcast(I32))
+        nc.sync.dma_start(out=sxw[:].bitcast(I32), in_=sx_words[0].bitcast(I32))
+        load_scales(nc.sync, wss, ws_scales)
+        load_scales(nc.sync, sxs, sx_scales)
+        nc.sync.dma_start(out=wbw[:], in_=wb_words[0].rearrange("p c r -> p (c r)").bitcast(I32))
+        load_scales(nc.sync, wbs, wb_scales)
+        nc.sync.dma_start(lists["l7"][:], offs7)
+        slope = tile("slope", [P, 2], F32)
+        shift = tile("shift", [P, 2], F32)
+        with nc.allow_non_contiguous_dma(reason="one value a partition"):
+            nc.sync.dma_start(out=slope[:], in_=so.rearrange("(h p) o -> p (h o)", p=P))
+            nc.sync.dma_start(out=shift[:], in_=bo.rearrange("(h p) o -> p (h o)", p=P))
+        tzt = [tile("tz%d" % h, [P, E], F32) for h in range(2)]
+        for h in range(2):
+            nc.sync.dma_start(out=tzt[h][:], in_=tz[h * P : (h + 1) * P, :])
+
+        aw, bw = tile("aw", [P, J], U32), tile("bw", [P, J], U32)
+        asc, bsc = tile("asc", [P, J], U8), tile("bsc", [P, J], U8)
+        wd = tile("wd", [P, R], U16)
+        wds = tile("wds", [P, R], U8)
+        nc.vector.tensor_copy(out=wd[:].rearrange("p (t m) -> p t m", t=PACK), in_=ww[:].rearrange("p (m t) -> p t m", t=PACK))
+        nc.vector.tensor_copy(asc[:], xs[:].indirect(lists["l1"][:]))
+        nc.vector.tensor_copy(bsc[:], xs[:].indirect(lists["l2"][:]))
+        nc.vector.tensor_copy(out=wds[:].rearrange("p (t m) -> p t m", t=PACK), in_=wsc[:].rearrange("p (m t) -> p t m", t=PACK))
+        nc.vector.tensor_copy(aw[:], xw[:].bitcast(U32).indirect(lists["l1"][:]))
+        nc.vector.tensor_copy(bw[:], xw[:].bitcast(U32).indirect(lists["l2"][:]))
+
+        def first_stage(acc, t, words, scales):
+            cols = slice(t * P, (t + 1) * P)
+            nc.tensor.matmul_mx(out=acc, lhsT=wd[:, cols].bitcast(E2M1), lhsT_scale=wds[:, cols],
+                                rhs=words[:].bitcast(E4M3), rhs_scale=scales[:], start=True, stop=True)
+
+        a_ps = [ps.tile([P, J], F32, name="a_ps%d" % t) for t in range(PACK)]
+        b_ps = [ps.tile([P, 2, J], F32, name="b_ps%d" % u) for u in range(2)]
+        for t in (0, 2, 1, 3):
+            first_stage(a_ps[t][:], t, aw, asc)
+        for t in range(PACK):
+            first_stage(b_ps[t // 2][:, t % 2, :], t, bw, bsc)
+
+        p_ps = [ps.tile([P, O], F32, name="p_ps%d" % h) for h in range(2)]
+        for h in range(2):
+            cols = slice(h * P, (h + 1) * P)
+            nc.tensor.matmul_mx(out=p_ps[h][:], lhsT=wsw[:, cols].bitcast(E5M2), lhsT_scale=wss[:, cols],
+                                rhs=sxw[:].bitcast(E2M1), rhs_scale=sxs, start=True, stop=False)
+
+        a_sb = [tile("a_sb%d" % t, [P, J], F32) for t in range(PACK)]
+        b_sb = [tile("b_sb%d" % u, [P, 2, J], F32) for u in range(2)]
+        gw = [tile("gw%d" % t, [P, O], F32) for t in range(PACK)]
+        diff = [tile("diff%d" % u, [P, 2, O], F32) for u in range(2)]
+        hid = tile("hid", [P, O, PACK], BF16)
+
+        def s_move(dst, src):
+            nc.scalar.activation(out=dst, in_=src, func=ACT.Copy)
+
+        def v_move(dst, src):
+            nc.vector.tensor_copy(out=dst, in_=src)
+
+        for u, move in ((0, s_move), (1, v_move)):
+            t0, t1 = 2 * u, 2 * u + 1
+            move(a_sb[t0][:], a_ps[t0][:])
+            move(a_sb[t1][:], a_ps[t1][:])
+            move(pw[t0][:].indirect(lists["l3"][:]), a_sb[t0][:])
+            move(b_sb[u][:], b_ps[u][:])
+            move(pw[t1][:].indirect(lists["l3"][:]), a_sb[t1][:])
+        for t in (0, 2, 1, 3):
+            s_move(gw[t][:], pw[t][:].indirect(lists["l5"][:]))
+        for u, move in ((0, s_move), (1, v_move)):
+            for i in range(2):
+                move(pv[2 * u + i][:].indirect(lists["l4"][:]), b_sb[u][:, i, :])
+        for u in (1, 0):
+            for i in range(2):
+                t = 2 * u + i
+                nc.vector.tensor_tensor(diff[u][:, i, :], pv[t][:].indirect(lists["l6"][:]), gw[t][:], ALU.subtract)
+        half = O // 2
+        nc.scalar.activation(out=hid[:, :, 2:4], in_=diff[1][:].rearrange("p t o -> p o t"), func=ACT.Abs)
+        nc.scalar.activation(out=hid[:, :half, 0:2], in_=diff[0][:, :, :half].rearrange("p t o -> p o t"), func=ACT.Abs)
+        last = diff[0][:, :, half:].rearrange("p t o -> p o t")
+        nc.vector.scalar_tensor_tensor(out=hid[:, half:, 0:2], in0=last, scalar=-1.0, in1=last, op0=ALU.mult, op1=ALU.max)
+
+        hq = tile("hq", [P, O], U32)
+        hs = tile("hs", [P, O], U8)
+        nc.vector.quantize_mx(out=hq[:].bitcast(E4M3), scales=hs[:], in_=hid[:].rearrange("p o t -> p (o t)"))
+
+        for h in range(2):
+            cols = slice(h * P, (h + 1) * P)
+            nc.tensor.matmul_mx(out=p_ps[h][:], lhsT=wbw[:, cols].bitcast(E5M2), lhsT_scale=wbs[:, cols],
+                                rhs=hq[:].bitcast(E4M3), rhs_scale=hs[:], start=False, stop=True)
+        for h, queue in ((0, nc.sync), (1, nc.scalar)):
+            gate = tile("gate%d" % h, [P, O], F32)
+            nc.scalar.activation(out=gate[:], in_=tzt[h][:].indirect(lists["l7"][:]), func=ACT.Sigmoid,
+                                 bias=shift[:, h : h + 1], scale=slope[:, h : h + 1])
+            res = tile("res%d" % h, [P, O], F32)
+            nc.vector.tensor_tensor(res[:], p_ps[h][:], gate[:], ALU.mult)
+            queue.dma_start(out=out[h * P : (h + 1) * P, :], in_=res[:])

@@ -57,18 +57,33 @@ def tile_list_tied_twoboards_skip_finalgate_kernel(
 
         pw = [tile("pw%d" % t, [P, C], F32) for t in range(PACK)]
         pv = [tile("pv%d" % t, [P, C], F32) for t in range(PACK)]
-        for board in pw[:2]:
+        for board in pv[2:]:
+            nc.gpsimd.memset(board[:], 0.0)
+        for board in pw[:3]:
             nc.vector.memset(board[:], 0.0)
         nc.vector.memset(late[:].bitcast(I32), 0)
         nc.vector.memset(wsc[:].bitcast(I32), 0)
-        for board in pw[2:] + pv:
+        warm = tile("warm", [P, 2], F32)
+        nc.vector.memset(warm[:, 0:1], 0.0)
+        for board in pw[3:] + pv[:2]:
             nc.vector.memset(board[:], 0.0)
 
         load_scales(nc.scalar, wsc, w_scales)
+        nc.scalar.activation(out=warm[:, 1:2], in_=warm[:, 0:1], func=ACT.Sigmoid)
         nc.sync.dma_start(lists["l3"][:], offs3)
         nc.sync.dma_start(lists["l5"][:], offs5)
         nc.sync.dma_start(lists["l4"][:], offs4)
         nc.sync.dma_start(lists["l6"][:], offs6)
+
+        nc.sync.dma_start(lists["l7"][:], offs7)
+        slope = tile("slope", [P, 2], F32)
+        shift = tile("shift", [P, 2], F32)
+        with nc.allow_non_contiguous_dma(reason="one value a partition"):
+            nc.sync.dma_start(out=slope[:], in_=so.rearrange("(h p) o -> p (h o)", p=P))
+            nc.sync.dma_start(out=shift[:], in_=bo.rearrange("(h p) o -> p (h o)", p=P))
+        tzt = [tile("tz%d" % h, [P, E], F32) for h in range(2)]
+        for h in range(2):
+            nc.sync.dma_start(out=tzt[h][:], in_=tz[h * P : (h + 1) * P, :])
 
         wsw = tile("wsw", [P, N], I32)
         sxw = tile("sxw", [P, O], U16)
@@ -80,50 +95,45 @@ def tile_list_tied_twoboards_skip_finalgate_kernel(
         load_scales(nc.sync, sxs, sx_scales)
         nc.sync.dma_start(out=wbw[:], in_=wb_words[0].rearrange("p c r -> p (c r)").bitcast(I32))
         load_scales(nc.sync, wbs, wb_scales)
-        nc.sync.dma_start(lists["l7"][:], offs7)
-        slope = tile("slope", [P, 2], F32)
-        shift = tile("shift", [P, 2], F32)
-        with nc.allow_non_contiguous_dma(reason="one value a partition"):
-            nc.sync.dma_start(out=slope[:], in_=so.rearrange("(h p) o -> p (h o)", p=P))
-            nc.sync.dma_start(out=shift[:], in_=bo.rearrange("(h p) o -> p (h o)", p=P))
-        tzt = [tile("tz%d" % h, [P, E], F32) for h in range(2)]
-        for h in range(2):
-            nc.sync.dma_start(out=tzt[h][:], in_=tz[h * P : (h + 1) * P, :])
 
         aw, bw = tile("aw", [P, J], U32), tile("bw", [P, J], U32)
         asc, bsc = tile("asc", [P, J], U8), tile("bsc", [P, J], U8)
         wd = tile("wd", [P, R], U16)
-        wds = tile("wds", [P, R], U8)
-        nc.vector.tensor_copy(out=wd[:].rearrange("p (t m) -> p t m", t=PACK), in_=ww[:].rearrange("p (m t) -> p t m", t=PACK))
+        wds = [tile("wds%d" % u, [P, 2, P], U8) for u in range(2)]
+        nc.scalar.copy(out=wd[:].rearrange("p (t m) -> p t m", t=PACK), in_=ww[:].rearrange("p (m t) -> p t m", t=PACK))
         nc.vector.tensor_copy(asc[:], xs[:].indirect(lists["l1"][:]))
         nc.vector.tensor_copy(bsc[:], xs[:].indirect(lists["l2"][:]))
-        nc.vector.tensor_copy(out=wds[:].rearrange("p (t m) -> p t m", t=PACK), in_=wsc[:].rearrange("p (m t) -> p t m", t=PACK))
         nc.vector.tensor_copy(aw[:], xw[:].bitcast(U32).indirect(lists["l1"][:]))
+        for u in range(2):
+            nc.vector.tensor_copy(out=wds[u][:], in_=wsc[:].rearrange("p (m t) -> p t m", t=PACK)[:, 2 * u : 2 * u + 2, :])
         nc.vector.tensor_copy(bw[:], xw[:].bitcast(U32).indirect(lists["l2"][:]))
 
         def first_stage(acc, t, words, scales):
             cols = slice(t * P, (t + 1) * P)
-            nc.tensor.matmul_mx(out=acc, lhsT=wd[:, cols].bitcast(E2M1), lhsT_scale=wds[:, cols],
+            nc.tensor.matmul_mx(out=acc, lhsT=wd[:, cols].bitcast(E2M1), lhsT_scale=wds[t // 2][:, t % 2, :],
                                 rhs=words[:].bitcast(E4M3), rhs_scale=scales[:], start=True, stop=True)
 
         a_ps = [ps.tile([P, J], F32, name="a_ps%d" % t) for t in range(PACK)]
         b_ps = [ps.tile([P, 2, J], F32, name="b_ps%d" % u) for u in range(2)]
-        for t in (0, 2, 1, 3):
+        for t in range(PACK):
             first_stage(a_ps[t][:], t, aw, asc)
         for t in range(PACK):
             first_stage(b_ps[t // 2][:, t % 2, :], t, bw, bsc)
 
-        p_ps = [ps.tile([P, O], F32, name="p_ps%d" % h) for h in range(2)]
-        for h in range(2):
-            cols = slice(h * P, (h + 1) * P)
-            nc.tensor.matmul_mx(out=p_ps[h][:], lhsT=wsw[:, cols].bitcast(E5M2), lhsT_scale=wss[:, cols],
-                                rhs=sxw[:].bitcast(E2M1), rhs_scale=sxs, start=True, stop=False)
+        half = O // 2
+        p_ps = [ps.tile([P, 2, half], F32, name="p_ps%d" % c) for c in range(2)]
+        for c in range(2):
+            reads = slice(c * half, (c + 1) * half)
+            for h in range(2):
+                cols = slice(h * P, (h + 1) * P)
+                nc.tensor.matmul_mx(out=p_ps[c][:, h, :], lhsT=wsw[:, cols].bitcast(E5M2), lhsT_scale=wss[:, cols],
+                                    rhs=sxw[:, reads].bitcast(E2M1), rhs_scale=sxs[:, reads], start=(h == 0), stop=False)
 
         a_sb = [tile("a_sb%d" % t, [P, J], F32) for t in range(PACK)]
-        b_sb = [tile("b_sb%d" % u, [P, 2, J], F32) for u in range(2)]
+        b_sb = [sb.tile([P, 2, J], F32, name="b_sb%d" % u, tag="b_sb%d" % u, align_bytes=64) for u in range(2)]
         gw = [tile("gw%d" % t, [P, O], F32) for t in range(PACK)]
         diff = [tile("diff%d" % u, [P, 2, O], F32) for u in range(2)]
-        hid = tile("hid", [P, O, PACK], BF16)
+        hid = [tile("hid%d" % c, [P, half, PACK], BF16) for c in range(2)]
 
         def s_move(dst, src):
             nc.scalar.activation(out=dst, in_=src, func=ACT.Copy)
@@ -143,28 +153,47 @@ def tile_list_tied_twoboards_skip_finalgate_kernel(
         for u, move in ((0, s_move), (1, v_move)):
             for i in range(2):
                 move(pv[2 * u + i][:].indirect(lists["l4"][:]), b_sb[u][:, i, :])
-        for u in (1, 0):
-            for i in range(2):
-                t = 2 * u + i
-                nc.vector.tensor_tensor(diff[u][:, i, :], pv[t][:].indirect(lists["l6"][:]), gw[t][:], ALU.subtract)
-        half = O // 2
-        nc.scalar.activation(out=hid[:, :, 2:4], in_=diff[1][:].rearrange("p t o -> p o t"), func=ACT.Abs)
-        nc.scalar.activation(out=hid[:, :half, 0:2], in_=diff[0][:, :, :half].rearrange("p t o -> p o t"), func=ACT.Abs)
-        last = diff[0][:, :, half:].rearrange("p t o -> p o t")
-        nc.vector.scalar_tensor_tensor(out=hid[:, half:, 0:2], in0=last, scalar=-1.0, in1=last, op0=ALU.mult, op1=ALU.max)
 
-        hq = tile("hq", [P, O], U32)
-        hs = tile("hs", [P, O], U8)
-        nc.vector.quantize_mx(out=hq[:].bitcast(E4M3), scales=hs[:], in_=hid[:].rearrange("p o t -> p (o t)"))
+        def difference(t, c0, c1):
+            nc.vector.tensor_tensor(diff[t // 2][:, t % 2, c0:c1], pv[t][:].indirect(lists["l6"][:, c0 // 16 : c1 // 16]), gw[t][:, c0:c1], ALU.subtract)
 
-        for h in range(2):
-            cols = slice(h * P, (h + 1) * P)
-            nc.tensor.matmul_mx(out=p_ps[h][:], lhsT=wbw[:, cols].bitcast(E5M2), lhsT_scale=wbs[:, cols],
-                                rhs=hq[:].bitcast(E4M3), rhs_scale=hs[:], start=False, stop=True)
-        for h, queue in ((0, nc.sync), (1, nc.scalar)):
-            gate = tile("gate%d" % h, [P, O], F32)
-            nc.scalar.activation(out=gate[:], in_=tzt[h][:].indirect(lists["l7"][:]), func=ACT.Sigmoid,
+        def magnitude_scalar(u):
+            src = diff[u][:, :, :half].rearrange("p t o -> p o t")
+            nc.scalar.activation(out=hid[0][:, :, 2 * u : 2 * u + 2], in_=src, func=ACT.Abs)
+
+        def magnitude_vector(u):
+            src = diff[u][:, :, half:].rearrange("p t o -> p o t")
+            nc.vector.scalar_tensor_tensor(out=hid[1][:, :, 2 * u : 2 * u + 2], in0=src, scalar=-1.0, in1=src, op0=ALU.mult, op1=ALU.max)
+
+        gate = sb.tile([P, 2, O], F32, name="gate", tag="b_sb0", align_bytes=64)
+
+        def final_gate(h):
+            nc.scalar.activation(out=gate[:, h, :], in_=tzt[h][:].indirect(lists["l7"][:]), func=ACT.Sigmoid,
                                  bias=shift[:, h : h + 1], scale=slope[:, h : h + 1])
-            res = tile("res%d" % h, [P, O], F32)
-            nc.vector.tensor_tensor(res[:], p_ps[h][:], gate[:], ALU.mult)
-            queue.dma_start(out=out[h * P : (h + 1) * P, :], in_=res[:])
+
+        for t in (2, 3, 0):
+            difference(t, 0, O)
+        magnitude_scalar(1)
+        magnitude_vector(1)
+        final_gate(0)
+        difference(1, 0, half)
+        difference(1, half, O)
+        magnitude_scalar(0)
+        magnitude_vector(0)
+        final_gate(1)
+
+        out_by_half = out.rearrange("(h p) o -> p h o", p=P)
+        for c, queue in ((0, nc.sync), (1, nc.scalar)):
+            reads = slice(c * half, (c + 1) * half)
+            hq = tile("hq%d" % c, [P, half], U32)
+            hs = tile("hs%d" % c, [P, half], U8)
+            nc.vector.quantize_mx(out=hq[:].bitcast(E4M3), scales=hs[:], in_=hid[c][:].rearrange("p o t -> p (o t)"))
+            for h in range(2):
+                cols = slice(h * P, (h + 1) * P)
+                nc.tensor.matmul_mx(out=p_ps[c][:, h, :], lhsT=wbw[:, cols].bitcast(E5M2), lhsT_scale=wbs[:, cols],
+                                    rhs=hq[:].bitcast(E4M3), rhs_scale=hs[:], start=False, stop=(h == 1))
+        for c, queue in ((0, nc.sync), (1, nc.scalar)):
+            reads = slice(c * half, (c + 1) * half)
+            res = tile("res%d" % c, [P, 2, half], F32)
+            nc.vector.tensor_tensor(res[:], p_ps[c][:], gate[:, :, reads], ALU.mult)
+            queue.dma_start(out=out_by_half[:, :, reads], in_=res[:])

@@ -57,15 +57,13 @@ def tile_list_tied_twoboards_skip_finalgate_kernel(
 
         pw = [tile("pw%d" % t, [P, C], F32) for t in range(PACK)]
         pv = [tile("pv%d" % t, [P, C], F32) for t in range(PACK)]
-        for board in pv[2:]:
-            nc.gpsimd.memset(board[:], 0.0)
         for board in pw[:3]:
             nc.vector.memset(board[:], 0.0)
         nc.vector.memset(late[:].bitcast(I32), 0)
         nc.vector.memset(wsc[:].bitcast(I32), 0)
         warm = tile("warm", [P, 2], F32)
         nc.vector.memset(warm[:, 0:1], 0.0)
-        for board in pw[3:] + pv[:2]:
+        for board in pw[3:] + pv:
             nc.vector.memset(board[:], 0.0)
 
         load_scales(nc.scalar, wsc, w_scales)
@@ -100,7 +98,7 @@ def tile_list_tied_twoboards_skip_finalgate_kernel(
         asc, bsc = tile("asc", [P, J], U8), tile("bsc", [P, J], U8)
         wd = tile("wd", [P, R], U16)
         wds = [tile("wds%d" % u, [P, 2, P], U8) for u in range(2)]
-        nc.scalar.copy(out=wd[:].rearrange("p (t m) -> p t m", t=PACK), in_=ww[:].rearrange("p (m t) -> p t m", t=PACK))
+        nc.vector.tensor_copy(out=wd[:].rearrange("p (t m) -> p t m", t=PACK), in_=ww[:].rearrange("p (m t) -> p t m", t=PACK))
         nc.vector.tensor_copy(asc[:], xs[:].indirect(lists["l1"][:]))
         nc.vector.tensor_copy(bsc[:], xs[:].indirect(lists["l2"][:]))
         nc.vector.tensor_copy(aw[:], xw[:].bitcast(U32).indirect(lists["l1"][:]))
@@ -121,13 +119,11 @@ def tile_list_tied_twoboards_skip_finalgate_kernel(
             first_stage(b_ps[t // 2][:, t % 2, :], t, bw, bsc)
 
         half = O // 2
-        p_ps = [ps.tile([P, 2, half], F32, name="p_ps%d" % c) for c in range(2)]
-        for c in range(2):
-            reads = slice(c * half, (c + 1) * half)
-            for h in range(2):
-                cols = slice(h * P, (h + 1) * P)
-                nc.tensor.matmul_mx(out=p_ps[c][:, h, :], lhsT=wsw[:, cols].bitcast(E5M2), lhsT_scale=wss[:, cols],
-                                    rhs=sxw[:, reads].bitcast(E2M1), rhs_scale=sxs[:, reads], start=(h == 0), stop=False)
+        p_ps = [ps.tile([P, O], F32, name="p_ps%d" % h) for h in range(2)]
+        for h in range(2):
+            cols = slice(h * P, (h + 1) * P)
+            nc.tensor.matmul_mx(out=p_ps[h][:], lhsT=wsw[:, cols].bitcast(E5M2), lhsT_scale=wss[:, cols],
+                                rhs=sxw[:].bitcast(E2M1), rhs_scale=sxs, start=True, stop=False)
 
         a_sb = [tile("a_sb%d" % t, [P, J], F32) for t in range(PACK)]
         b_sb = [sb.tile([P, 2, J], F32, name="b_sb%d" % u, tag="b_sb%d" % u, align_bytes=64) for u in range(2)]
@@ -148,22 +144,19 @@ def tile_list_tied_twoboards_skip_finalgate_kernel(
             move(pw[t0][:].indirect(lists["l3"][:]), a_sb[t0][:])
             move(b_sb[u][:], b_ps[u][:])
             move(pw[t1][:].indirect(lists["l3"][:]), a_sb[t1][:])
-        for t in (0, 2, 1, 3):
+        for t in (0, 2, 1):
             s_move(gw[t][:], pw[t][:].indirect(lists["l5"][:]))
         for u, move in ((0, s_move), (1, v_move)):
             for i in range(2):
                 move(pv[2 * u + i][:].indirect(lists["l4"][:]), b_sb[u][:, i, :])
+        v_move(gw[3][:], pw[3][:].indirect(lists["l5"][:]))
 
         def difference(t, c0, c1):
             nc.vector.tensor_tensor(diff[t // 2][:, t % 2, c0:c1], pv[t][:].indirect(lists["l6"][:, c0 // 16 : c1 // 16]), gw[t][:, c0:c1], ALU.subtract)
 
-        def magnitude_scalar(u):
-            src = diff[u][:, :, :half].rearrange("p t o -> p o t")
-            nc.scalar.activation(out=hid[0][:, :, 2 * u : 2 * u + 2], in_=src, func=ACT.Abs)
-
-        def magnitude_vector(u):
-            src = diff[u][:, :, half:].rearrange("p t o -> p o t")
-            nc.vector.scalar_tensor_tensor(out=hid[1][:, :, 2 * u : 2 * u + 2], in0=src, scalar=-1.0, in1=src, op0=ALU.mult, op1=ALU.max)
+        def magnitude(u, c):
+            src = diff[u][:, :, c * half : (c + 1) * half].rearrange("p t o -> p o t")
+            nc.scalar.activation(out=hid[c][:, :, 2 * u : 2 * u + 2], in_=src, func=ACT.Abs)
 
         gate = sb.tile([P, 2, O], F32, name="gate", tag="b_sb0", align_bytes=64)
 
@@ -173,27 +166,25 @@ def tile_list_tied_twoboards_skip_finalgate_kernel(
 
         for t in (2, 3, 0):
             difference(t, 0, O)
-        magnitude_scalar(1)
-        magnitude_vector(1)
+        magnitude(1, 0)
+        magnitude(1, 1)
         final_gate(0)
         difference(1, 0, half)
         difference(1, half, O)
-        magnitude_scalar(0)
-        magnitude_vector(0)
+        magnitude(0, 0)
+        magnitude(0, 1)
         final_gate(1)
 
-        out_by_half = out.rearrange("(h p) o -> p h o", p=P)
-        for c, queue in ((0, nc.sync), (1, nc.scalar)):
+        for c in range(2):
             reads = slice(c * half, (c + 1) * half)
             hq = tile("hq%d" % c, [P, half], U32)
             hs = tile("hs%d" % c, [P, half], U8)
             nc.vector.quantize_mx(out=hq[:].bitcast(E4M3), scales=hs[:], in_=hid[c][:].rearrange("p o t -> p (o t)"))
             for h in range(2):
                 cols = slice(h * P, (h + 1) * P)
-                nc.tensor.matmul_mx(out=p_ps[c][:, h, :], lhsT=wbw[:, cols].bitcast(E5M2), lhsT_scale=wbs[:, cols],
-                                    rhs=hq[:].bitcast(E4M3), rhs_scale=hs[:], start=False, stop=(h == 1))
-        for c, queue in ((0, nc.sync), (1, nc.scalar)):
-            reads = slice(c * half, (c + 1) * half)
-            res = tile("res%d" % c, [P, 2, half], F32)
-            nc.vector.tensor_tensor(res[:], p_ps[c][:], gate[:, :, reads], ALU.mult)
-            queue.dma_start(out=out_by_half[:, :, reads], in_=res[:])
+                nc.tensor.matmul_mx(out=p_ps[h][:, reads], lhsT=wbw[:, cols].bitcast(E5M2), lhsT_scale=wbs[:, cols],
+                                    rhs=hq[:].bitcast(E4M3), rhs_scale=hs[:], start=False, stop=(c == 1))
+        for h, queue in ((0, nc.sync), (1, nc.scalar)):
+            res = tile("res%d" % h, [P, O], F32)
+            nc.vector.tensor_tensor(res[:], p_ps[h][:], gate[:, h, :], ALU.mult)
+            queue.dma_start(out=out[h * P : (h + 1) * P, :], in_=res[:])

@@ -129,7 +129,7 @@ def tile_list_tied_twoboards_skip_finalgate_kernel(
         b_sb = [sb.tile([P, 2, J], F32, name="b_sb%d" % u, tag="b_sb%d" % u, align_bytes=64) for u in range(2)]
         gw = [tile("gw%d" % t, [P, O], F32) for t in range(PACK)]
         diff = [tile("diff%d" % u, [P, 2, O], F32) for u in range(2)]
-        hid = [tile("hid%d" % c, [P, half, PACK], BF16) for c in range(2)]
+        hid = tile("hid", [P, O, PACK], BF16)
 
         def s_move(dst, src):
             nc.scalar.activation(out=dst, in_=src, func=ACT.Copy)
@@ -137,26 +137,26 @@ def tile_list_tied_twoboards_skip_finalgate_kernel(
         def v_move(dst, src):
             nc.vector.tensor_copy(out=dst, in_=src)
 
+        s_move(a_sb[0][:], a_ps[0][:])
+        for t in (2, 1, 3):
+            v_move(a_sb[t][:], a_ps[t][:])
         for u, move in ((0, s_move), (1, v_move)):
             t0, t1 = 2 * u, 2 * u + 1
-            move(a_sb[t0][:], a_ps[t0][:])
-            move(a_sb[t1][:], a_ps[t1][:])
             move(pw[t0][:].indirect(lists["l3"][:]), a_sb[t0][:])
             move(b_sb[u][:], b_ps[u][:])
             move(pw[t1][:].indirect(lists["l3"][:]), a_sb[t1][:])
-        for t in (0, 2, 1):
+        for t in (0, 2, 1, 3):
             s_move(gw[t][:], pw[t][:].indirect(lists["l5"][:]))
         for u, move in ((0, s_move), (1, v_move)):
             for i in range(2):
                 move(pv[2 * u + i][:].indirect(lists["l4"][:]), b_sb[u][:, i, :])
-        v_move(gw[3][:], pw[3][:].indirect(lists["l5"][:]))
 
         def difference(t, c0, c1):
             nc.vector.tensor_tensor(diff[t // 2][:, t % 2, c0:c1], pv[t][:].indirect(lists["l6"][:, c0 // 16 : c1 // 16]), gw[t][:, c0:c1], ALU.subtract)
 
-        def magnitude(u, c):
-            src = diff[u][:, :, c * half : (c + 1) * half].rearrange("p t o -> p o t")
-            nc.scalar.activation(out=hid[c][:, :, 2 * u : 2 * u + 2], in_=src, func=ACT.Abs)
+        def magnitude(u, c0, c1):
+            src = diff[u][:, :, c0:c1].rearrange("p t o -> p o t")
+            nc.scalar.activation(out=hid[:, c0:c1, 2 * u : 2 * u + 2], in_=src, func=ACT.Abs)
 
         gate = sb.tile([P, 2, O], F32, name="gate", tag="b_sb0", align_bytes=64)
 
@@ -166,20 +166,19 @@ def tile_list_tied_twoboards_skip_finalgate_kernel(
 
         for t in (2, 3, 0):
             difference(t, 0, O)
-        magnitude(1, 0)
-        magnitude(1, 1)
+        magnitude(1, 0, O)
         final_gate(0)
         difference(1, 0, half)
         difference(1, half, O)
-        magnitude(0, 0)
-        magnitude(0, 1)
+        magnitude(0, 0, half)
+        magnitude(0, half, O)
         final_gate(1)
 
         for c in range(2):
             reads = slice(c * half, (c + 1) * half)
             hq = tile("hq%d" % c, [P, half], U32)
             hs = tile("hs%d" % c, [P, half], U8)
-            nc.vector.quantize_mx(out=hq[:].bitcast(E4M3), scales=hs[:], in_=hid[c][:].rearrange("p o t -> p (o t)"))
+            nc.vector.quantize_mx(out=hq[:].bitcast(E4M3), scales=hs[:], in_=hid[:, reads, :].rearrange("p o t -> p (o t)"))
             for h in range(2):
                 cols = slice(h * P, (h + 1) * P)
                 nc.tensor.matmul_mx(out=p_ps[h][:, reads], lhsT=wbw[:, cols].bitcast(E5M2), lhsT_scale=wbs[:, cols],

from contextlib import ExitStack

import concourse.mybir as mybir

K, T, J, R, C, O, N, L, E = 512, 2048, 256, 512, 512, 256, 256, 512, 1024
FLOPS = 2 * (2 * K * R * J + R * N * O + L * N * O)

F32 = mybir.dt.float32
BF16 = mybir.dt.bfloat16
I32 = mybir.dt.int32
U32 = mybir.dt.uint32
U16 = mybir.dt.uint16
U8 = mybir.dt.uint8
E4M3 = mybir.dt.float8_e4m3fn_x4
E5M2 = mybir.dt.float8_e5m2_x4
E2M1 = mybir.dt.float4_e2m1fn_x4
ACT = mybir.ActivationFunctionType
ALU = mybir.AluOpType

P = 128
PACK = 4
QUADS = 4


def load_scales(queue, plane, scales, quads=range(QUADS)):
    for q in quads:
        queue.dma_start(out=plane[32 * q : 32 * q + 4, :].bitcast(I32), in_=scales[0, 4 * q : 4 * q + 4, :].bitcast(I32))


def tile_list_tied_twoboards_skip_finalgate_kernel(
    tc, xt_words, xt_scales, w_words, w_scales, wb_words, wb_scales, sx_words, sx_scales, ws_words, ws_scales,
    tz, so, bo, offs, offs2, offs3, offs4, offs5, offs6, offs7, out,
):
    nc = tc.nc
    with ExitStack() as ctx:
        sb = ctx.enter_context(tc.tile_pool(name="sb", bufs=1))
        ps = ctx.enter_context(tc.psum_pool(name="ps", bufs=1))

        def tile(name, shape, dtype):
            return sb.tile(shape, dtype, name=name, align_bytes=64)

        lists = {n: tile(n, [P, J // 16], U16) for n in ("l1", "l2", "l3", "l4", "l5", "l6", "l7")}
        xw = tile("xw", [P, T], I32)
        xs = tile("xs", [P, T], U8)
        ww = tile("ww", [P, R], U16)
        wsc = tile("wsc", [P, R], U8)
        late = tile("late", [P, 3 * N], U8)

        nc.vector.memset(xs[:].bitcast(I32), 0)

        nc.sync.dma_start(lists["l1"][:], offs)
        nc.scalar.dma_start(out=ww[:].bitcast(I32), in_=w_words[0].bitcast(I32))
        nc.sync.dma_start(lists["l2"][:], offs2)
        load_scales(nc.scalar, xs, xt_scales, (0, 1))
        load_scales(nc.sync, xs, xt_scales, (2, 3))
        nc.sync.dma_start(out=xw[:], in_=xt_words[0].rearrange("p c r -> p (c r)").bitcast(I32))

        pw = [tile("pw%d" % t, [P, C], F32) for t in range(PACK)]
        pv = [tile("pv%d" % t, [P, C], F32) for t in range(PACK)]
        for board in pw[:3]:
            nc.vector.memset(board[:], 0.0)
        nc.vector.memset(late[:].bitcast(I32), 0)
        nc.vector.memset(wsc[:].bitcast(I32), 0)
        warm = tile("warm", [P, 2], F32)
        nc.vector.memset(warm[:, 0:1], 0.0)
        for board in pw[3:] + pv:
            nc.vector.memset(board[:], 0.0)

        load_scales(nc.scalar, wsc, w_scales)
        nc.scalar.activation(out=warm[:, 1:2], in_=warm[:, 0:1], func=ACT.Sigmoid)
        nc.sync.dma_start(lists["l3"][:], offs3)
        nc.sync.dma_start(lists["l5"][:], offs5)
        nc.sync.dma_start(lists["l4"][:], offs4)
        nc.sync.dma_start(lists["l6"][:], offs6)

        nc.sync.dma_start(lists["l7"][:], offs7)
        slope = tile("slope", [P, 2], F32)
        shift = tile("shift", [P, 2], F32)
        with nc.allow_non_contiguous_dma(reason="one value a partition"):
            nc.sync.dma_start(out=slope[:], in_=so.rearrange("(h p) o -> p (h o)", p=P))
            nc.sync.dma_start(out=shift[:], in_=bo.rearrange("(h p) o -> p (h o)", p=P))
        tzt = [tile("tz%d" % h, [P, E], F32) for h in range(2)]
        for h in range(2):
            nc.sync.dma_start(out=tzt[h][:], in_=tz[h * P : (h + 1) * P, :])

        wsw = tile("wsw", [P, N], I32)
        sxw = tile("sxw", [P, O], U16)
        wbw = tile("wbw", [P, N], I32)
        wss, sxs, wbs = late[:, 0:N], late[:, N : 2 * N], late[:, 2 * N : 3 * N]
        nc.sync.dma_start(out=wsw[:], in_=ws_words[0].rearrange("p c r -> p (c r)").bitcast(I32))
        nc.sync.dma_start(out=sxw[:].bitcast(I32), in_=sx_words[0].bitcast(I32))
        load_scales(nc.sync, wss, ws_scales)
        load_scales(nc.sync, sxs, sx_scales)
        nc.sync.dma_start(out=wbw[:], in_=wb_words[0].rearrange("p c r -> p (c r)").bitcast(I32))
        load_scales(nc.sync, wbs, wb_scales)

        aw, bw = tile("aw", [P, J], U32), tile("bw", [P, J], U32)
        asc, bsc = tile("asc", [P, J], U8), tile("bsc", [P, J], U8)
        wd = tile("wd", [P, R], U16)
        wds = [tile("wds%d" % u, [P, 2, P], U8) for u in range(2)]
        nc.vector.tensor_copy(out=wd[:].rearrange("p (t m) -> p t m", t=PACK), in_=ww[:].rearrange("p (m t) -> p t m", t=PACK))
        nc.vector.tensor_copy(asc[:], xs[:].indirect(lists["l1"][:]))
        nc.vector.tensor_copy(bsc[:], xs[:].indirect(lists["l2"][:]))
        nc.vector.tensor_copy(aw[:], xw[:].bitcast(U32).indirect(lists["l1"][:]))
        for u in range(2):
            nc.vector.tensor_copy(out=wds[u][:], in_=wsc[:].rearrange("p (m t) -> p t m", t=PACK)[:, 2 * u : 2 * u + 2, :])
        nc.vector.tensor_copy(bw[:], xw[:].bitcast(U32).indirect(lists["l2"][:]))

        def first_stage(acc, t, words, scales):
            cols = slice(t * P, (t + 1) * P)
            nc.tensor.matmul_mx(out=acc, lhsT=wd[:, cols].bitcast(E2M1), lhsT_scale=wds[t // 2][:, t % 2, :],
                                rhs=words[:].bitcast(E4M3), rhs_scale=scales[:], start=True, stop=True)

        a_ps = [ps.tile([P, J], F32, name="a_ps%d" % t) for t in range(PACK)]
        b_ps = [ps.tile([P, 2, J], F32, name="b_ps%d" % u) for u in range(2)]
        for t in range(PACK):
            first_stage(a_ps[t][:], t, aw, asc)
        for t in range(PACK):
            first_stage(b_ps[t // 2][:, t % 2, :], t, bw, bsc)

        half = O // 2
        p_ps = [ps.tile([P, O], F32, name="p_ps%d" % h) for h in range(2)]
        for h in range(2):
            cols = slice(h * P, (h + 1) * P)
            nc.tensor.matmul_mx(out=p_ps[h][:], lhsT=wsw[:, cols].bitcast(E5M2), lhsT_scale=wss[:, cols],
                                rhs=sxw[:].bitcast(E2M1), rhs_scale=sxs, start=True, stop=False)

        a_sb = [tile("a_sb%d" % t, [P, J], F32) for t in range(PACK)]
        b_sb = [sb.tile([P, 2, J], F32, name="b_sb%d" % u, tag="b_sb%d" % u, align_bytes=64) for u in range(2)]
        gw = [tile("gw%d" % t, [P, O], F32) for t in range(PACK)]
        diff = [tile("diff%d" % u, [P, 2, O], F32) for u in range(2)]
        hid = tile("hid", [P, O, PACK], BF16)

        def s_move(dst, src):
            nc.scalar.activation(out=dst, in_=src, func=ACT.Copy)

        def v_move(dst, src):
            nc.vector.tensor_copy(out=dst, in_=src)

        s_move(a_sb[0][:], a_ps[0][:])
        for t in (2, 1, 3):
            v_move(a_sb[t][:], a_ps[t][:])
        for u, move in ((0, s_move), (1, v_move)):
            t0, t1 = 2 * u, 2 * u + 1
            move(pw[t0][:].indirect(lists["l3"][:]), a_sb[t0][:])
            move(b_sb[u][:], b_ps[u][:])
            move(pw[t1][:].indirect(lists["l3"][:]), a_sb[t1][:])
        for t in (0, 2, 1, 3):
            s_move(gw[t][:], pw[t][:].indirect(lists["l5"][:]))
        for u, move in ((0, s_move), (1, v_move)):
            for i in range(2):
                move(pv[2 * u + i][:].indirect(lists["l4"][:]), b_sb[u][:, i, :])

        def difference(t, c0, c1):
            nc.vector.tensor_tensor(diff[t // 2][:, t % 2, c0:c1], pv[t][:].indirect(lists["l6"][:, c0 // 16 : c1 // 16]), gw[t][:, c0:c1], ALU.subtract)

        def magnitude(u, c0, c1):
            src = diff[u][:, :, c0:c1].rearrange("p t o -> p o t")
            nc.scalar.activation(out=hid[:, c0:c1, 2 * u : 2 * u + 2], in_=src, func=ACT.Abs)

        gate = sb.tile([P, 2, O], F32, name="gate", tag="b_sb0", align_bytes=64)

        def final_gate(h):
            nc.scalar.activation(out=gate[:, h, :], in_=tzt[h][:].indirect(lists["l7"][:]), func=ACT.Sigmoid,
                                 bias=shift[:, h : h + 1], scale=slope[:, h : h + 1])

        for t in (2, 3, 0):
            difference(t, 0, O)
        magnitude(1, 0, O)
        final_gate(0)
        difference(1, 0, half)
        difference(1, half, O)
        magnitude(0, 0, half)
        magnitude(0, half, O)
        final_gate(1)

        for c in range(2):
            reads = slice(c * half, (c + 1) * half)
            hq = tile("hq%d" % c, [P, half], U32)
            hs = tile("hs%d" % c, [P, half], U8)
            nc.vector.quantize_mx(out=hq[:].bitcast(E4M3), scales=hs[:], in_=hid[:, reads, :].rearrange("p o t -> p (o t)"))
            for h in range(2):
                cols = slice(h * P, (h + 1) * P)
                nc.tensor.matmul_mx(out=p_ps[h][:, reads], lhsT=wbw[:, cols].bitcast(E5M2), lhsT_scale=wbs[:, cols],
                                    rhs=hq[:].bitcast(E4M3), rhs_scale=hs[:], start=False, stop=(c == 1))
        for h, queue in ((0, nc.sync), (1, nc.scalar)):
            res = tile("res%d" % h, [P, O], F32)
            nc.vector.tensor_tensor(res[:], p_ps[h][:], gate[:, h, :], ALU.mult)
            queue.dma_start(out=out[h * P : (h + 1) * P, :], in_=res[:])
